import numpy as np
import ml_dtypes


def mxq(x, axis, fmt="e4m3"):
    dtype, down = {"e4m3": (ml_dtypes.float8_e4m3fn, 7), "e5m2": (ml_dtypes.float8_e5m2, 14)}[fmt]
    v = np.moveaxis(np.asarray(x, np.float32).astype(ml_dtypes.bfloat16).astype(np.float64), axis, -1)
    blocks = v.reshape(v.shape[:-1] + (-1, 32))
    amax = np.abs(blocks).max(-1, keepdims=True)
    byte = np.maximum(np.where(amax > 0, np.frexp(amax)[1] - 1 + 127, 0) - down, 1)
    scale = np.exp2(byte - 127.0)
    codes = (blocks / scale).astype(np.float32).astype(dtype).astype(np.float64)
    return np.moveaxis((codes * scale).reshape(v.shape), -1, axis)


WIDE = False


def mx_kscale(k):
    if not WIDE:
        return np.ones(k)
    levels = np.array([10, -10, 5, -5, 0])
    if k % 512:
        return np.exp2(np.random.permutation(np.resize(levels, k // 32))).repeat(32)
    a = np.empty((k // 512, 16))
    for p in range(k // 512):
        a[p, :8] = np.random.permutation(np.resize(levels, 8))
        for g in range(8):
            far = levels[np.abs(levels - a[p, g]) >= 10]
            a[p, g + 8] = far[np.random.randint(len(far))]
    return np.exp2(a.ravel()).repeat(32)


def f64(x):
    return np.asarray(x).astype(np.float64)


def striped(idx):
    return np.tile(idx.reshape(-1, 16).T, (8, 1)).astype(np.uint16)


def unstriped(offs):
    return offs[:16].T.reshape(-1).astype(np.int64)


K, T, D, S, V, N = 512, 1024, 4, 2048, 512, 512


def setup_inputs():
    n = np.random.standard_normal
    s = mx_kscale(K)[:, None]
    return {
        "xT": (n((K, T)) * s).astype(np.float32),
        "w": (n((K, N)) / np.sqrt(K) / s).astype(np.float32),
        "b": (0.3 * n((N, 1))).astype(np.float32),
        "offs": striped(np.concatenate([np.random.permutation(T)[:V] for _ in range(D)])),
    }


def reference(xT, w, b, offs):
    idx = unstriped(offs)
    x = np.empty((K, V))
    for l in range(D):
        r = l // 4 * (4 * K // D) + l % 4 + 4 * np.arange(K // D)
        x[r] = f64(xT)[r][:, idx[l * V:(l + 1) * V]]
    xq = mxq(x, 0, "e4m3")
    return (mxq(f64(w), 0, "e4m3").T @ xq) + f64(b)

@@ -1,0 +1,110 @@
+from contextlib import ExitStack
+
+import concourse.mybir as mybir
+
+K, T, LEVELS, V, N = 512, 1024, 4, 512, 512
+FLOPS = 2 * K * N * V
+
+F32 = mybir.dt.float32
+BF16 = mybir.dt.bfloat16
+U32 = mybir.dt.uint32
+U16 = mybir.dt.uint16
+U8 = mybir.dt.uint8
+FP8X4 = mybir.dt.float8_e4m3fn_x4
+ADD = mybir.AluOpType.add
+IDENTITY = mybir.ActivationFunctionType.Identity
+
+P = 128
+H = 256
+M = 128
+
+
+def tile_picked_grid_lin_bias_sub_l_kernel(tc, xT, w, b, offs, out):
+    nc = tc.nc
+    with ExitStack() as ctx:
+        lists = ctx.enter_context(tc.tile_pool(name="lists", bufs=1))
+        keep = ctx.enter_context(tc.tile_pool(name="keep", bufs=1))
+        psum = ctx.enter_context(tc.psum_pool(name="psum", bufs=1))
+
+        offsets = lists.tile([P, LEVELS * V // 16], U16, name="offsets")
+        nc.sync.dma_start(offsets[:], offs)
+
+        warm = keep.tile([P, 1], F32, name="warm")
+        nc.gpsimd.memset(warm[:], 0.0)
+        warm_out = keep.tile([P, 1], F32, name="warm_out")
+        nc.scalar.activation(warm_out[:], warm[:], IDENTITY)
+
+        x_levels = xT.rearrange("(f l) t -> l f t", l=LEVELS)
+        tables = []
+        for l in range(LEVELS):
+            table = keep.tile([P, T], F32, name=f"table{l}")
+            nc.sync.dma_start(table[:], x_levels[l])
+            tables.append(table)
+        w_raw = []
+        for h in range(2):
+            raw = keep.tile([P, 4, 2 * M], F32, name=f"w_raw{h}")
+            nc.sync.dma_start(raw[:], w[:, 2 * M * h : 2 * M * (h + 1)].rearrange("(p j) c -> p j c", j=4))
+            w_raw.append(raw)
+        bias = keep.tile([P, 4], F32, name="bias")
+        with nc.allow_non_contiguous_dma(reason="512 bias values, one DMA"):
+            nc.sync.dma_start(bias[:], b.rearrange("(c p) o -> p (c o)", p=P))
+
+        looked = [keep.tile([P, LEVELS, H], F32, name=f"looked{v}") for v in range(2)]
+        for l in range(LEVELS):
+            for v in range(2):
+                first = (V * l + H * v) // 16
+                nc.vector.tensor_copy(
+                    looked[v][:, l, :],
+                    tables[l][:].indirect(offsets[:, first : first + H // 16]),
+                )
+
+        def interleave(engine_copy, dst, src):
+            engine_copy(dst[:], src.rearrange("p j n -> p n j"))
+
+        x_grouped = [keep.tile([P, H, 4], BF16, name=f"x_grouped{v}", align_bytes=64) for v in range(2)]
+        x_codes = [keep.tile([P, H], U32, name=f"x_codes{v}", align_bytes=64) for v in range(2)]
+        x_scales = [keep.tile([P, H], U8, name=f"x_scales{v}", align_bytes=64) for v in range(2)]
+        w_grouped = [keep.tile([P, M, 4], BF16, name=f"w_grouped{m}", align_bytes=64) for m in range(4)]
+        w_codes = [keep.tile([P, M], U32, name=f"w_codes{m}", align_bytes=64) for m in range(4)]
+        w_scales = [keep.tile([P, M], U8, name=f"w_scales{m}", align_bytes=64) for m in range(4)]
+
+        def quantize(codes, scales, grouped):
+            nc.vector.quantize_mx(
+                out=codes[:].bitcast(FP8X4), scales=scales[:], in_=grouped[:].rearrange("p n j -> p (n j)")
+            )
+
+        def w_slice(m):
+            return w_raw[m // 2][:, :, M * (m % 2) : M * (m % 2 + 1)]
+
+        interleave(nc.scalar.copy, x_grouped[0], looked[0][:])
+        interleave(nc.vector.tensor_copy, x_grouped[1], looked[1][:])
+        interleave(nc.scalar.copy, w_grouped[0], w_slice(0))
+        interleave(nc.scalar.copy, w_grouped[1], w_slice(1))
+        quantize(x_codes[0], x_scales[0], x_grouped[0])
+        quantize(x_codes[1], x_scales[1], x_grouped[1])
+        quantize(w_codes[0], w_scales[0], w_grouped[0])
+        interleave(nc.vector.tensor_copy, w_grouped[2], w_slice(2))
+        quantize(w_codes[1], w_scales[1], w_grouped[1])
+        interleave(nc.vector.tensor_copy, w_grouped[3], w_slice(3))
+        quantize(w_codes[2], w_scales[2], w_grouped[2])
+        quantize(w_codes[3], w_scales[3], w_grouped[3])
+
+        for m in range(4):
+            result = keep.tile([P, V], F32, name=f"result{m}")
+            for v in range(2):
+                acc = psum.tile([P, H], F32, name=f"acc{m}{v}")
+                nc.tensor.matmul_mx(
+                    out=acc[:],
+                    lhsT=w_codes[m][:].bitcast(FP8X4),
+                    lhsT_scale=w_scales[m][:],
+                    rhs=x_codes[v][:].bitcast(FP8X4),
+                    rhs_scale=x_scales[v][:],
+                    start=True,
+                    stop=True,
+                )
+                part = result[:, H * v : H * (v + 1)]
+                if v == 0:
+                    nc.scalar.activation(part, acc[:], IDENTITY, bias=bias[:, m : m + 1])
+                else:
+                    nc.vector.tensor_scalar(part, acc[:], bias[:, m : m + 1], None, ADD)
+            nc.sync.dma_start(out[M * m : M * (m + 1), :], result[:])

@@ -1,6 +1,7 @@
 from contextlib import ExitStack
 
 import concourse.mybir as mybir
+from concourse.masks import make_identity
 
 K, T, LEVELS, V, N = 512, 1024, 4, 512, 512
 FLOPS = 2 * K * N * V
@@ -12,6 +13,7 @@ U16 = mybir.dt.uint16
 U8 = mybir.dt.uint8
 FP8X4 = mybir.dt.float8_e4m3fn_x4
 ADD = mybir.AluOpType.add
+MULT = mybir.AluOpType.mult
 IDENTITY = mybir.ActivationFunctionType.Identity
 
 P = 128
@@ -28,12 +30,6 @@ def tile_picked_grid_lin_bias_sub_l_kernel(tc, xT, w, b, offs, out):
 
         offsets = lists.tile([P, LEVELS * V // 16], U16, name="offsets")
         nc.sync.dma_start(offsets[:], offs)
-
-        warm = keep.tile([P, 1], F32, name="warm")
-        nc.gpsimd.memset(warm[:], 0.0)
-        warm_out = keep.tile([P, 1], F32, name="warm_out")
-        nc.scalar.activation(warm_out[:], warm[:], IDENTITY)
-
         x_levels = xT.rearrange("(f l) t -> l f t", l=LEVELS)
         tables = []
         for l in range(LEVELS):
@@ -45,66 +41,95 @@ def tile_picked_grid_lin_bias_sub_l_kernel(tc, xT, w, b, offs, out):
             raw = keep.tile([P, 4, 2 * M], F32, name=f"w_raw{h}")
             nc.sync.dma_start(raw[:], w[:, 2 * M * h : 2 * M * (h + 1)].rearrange("(p j) c -> p j c", j=4))
             w_raw.append(raw)
+
+        acc = [[psum.tile([P, H], F32, name=f"acc{m}{v}") for v in range(2)] for m in range(4)]
+
+        bias_rows = keep.tile([P, P], F32, name="bias_rows")
+        nc.gpsimd.memset(bias_rows[:], 0.0)
+        nc.scalar.dma_start(bias_rows[0:4, :], b.rearrange("(c m) o -> c (m o)", c=4))
+        identity = keep.tile([P, P], F32, name="identity")
+        make_identity(nc, identity[:])
+        nc.tensor.transpose(acc[3][1][:, 0:P], bias_rows[:], identity[:])
         bias = keep.tile([P, 4], F32, name="bias")
-        with nc.allow_non_contiguous_dma(reason="512 bias values, one DMA"):
-            nc.sync.dma_start(bias[:], b.rearrange("(c p) o -> p (c o)", p=P))
+        nc.scalar.activation(bias[:], acc[3][1][:, 0:4], IDENTITY)
 
-        looked = [keep.tile([P, LEVELS, H], F32, name=f"looked{v}") for v in range(2)]
-        for l in range(LEVELS):
-            for v in range(2):
-                first = (V * l + H * v) // 16
-                nc.vector.tensor_copy(
-                    looked[v][:, l, :],
-                    tables[l][:].indirect(offsets[:, first : first + H // 16]),
-                )
+        looked = [keep.tile([P, 2, V], F32, name=f"looked{i}") for i in range(2)]
 
-        def interleave(engine_copy, dst, src):
-            engine_copy(dst[:], src.rearrange("p j n -> p n j"))
+        def look_up(l, v0, v1):
+            first = (V * l + v0) // 16
+            last = (V * l + v1) // 16
+            nc.vector.tensor_copy(looked[l // 2][:, l % 2, v0:v1], tables[l][:].indirect(offsets[:, first:last]))
 
-        x_grouped = [keep.tile([P, H, 4], BF16, name=f"x_grouped{v}", align_bytes=64) for v in range(2)]
+        x_grouped = keep.tile([P, V, 4], BF16, name="x_grouped", align_bytes=64)
         x_codes = [keep.tile([P, H], U32, name=f"x_codes{v}", align_bytes=64) for v in range(2)]
         x_scales = [keep.tile([P, H], U8, name=f"x_scales{v}", align_bytes=64) for v in range(2)]
         w_grouped = [keep.tile([P, M, 4], BF16, name=f"w_grouped{m}", align_bytes=64) for m in range(4)]
         w_codes = [keep.tile([P, M], U32, name=f"w_codes{m}", align_bytes=64) for m in range(4)]
         w_scales = [keep.tile([P, M], U8, name=f"w_scales{m}", align_bytes=64) for m in range(4)]
 
+        def group_x(copy, i, v0, v1):
+            copy(x_grouped[:, v0:v1, 2 * i : 2 * i + 2], looked[i][:, :, v0:v1].rearrange("p j n -> p n j"))
+
+        def on_gpsimd(dst, src):
+            nc.gpsimd.tensor_scalar(dst, src, 1.0, 0.0, MULT, ADD)
+
+        def group_w(copy, m):
+            raw = w_raw[m // 2][:, :, M * (m % 2) : M * (m % 2 + 1)]
+            copy(w_grouped[m][:], raw.rearrange("p j n -> p n j"))
+
         def quantize(codes, scales, grouped):
-            nc.vector.quantize_mx(
-                out=codes[:].bitcast(FP8X4), scales=scales[:], in_=grouped[:].rearrange("p n j -> p (n j)")
+            nc.vector.quantize_mx(out=codes[:].bitcast(FP8X4), scales=scales[:], in_=grouped.rearrange("p n j -> p (n j)"))
+
+        def quantize_x(v):
+            quantize(x_codes[v], x_scales[v], x_grouped[:, H * v : H * (v + 1), :])
+
+        def quantize_w(m):
+            quantize(w_codes[m], w_scales[m], w_grouped[m][:])
+
+        def multiply(m, v, on_scalar):
+            nc.tensor.matmul_mx(
+                out=acc[m][v][:],
+                lhsT=w_codes[m][:].bitcast(FP8X4),
+                lhsT_scale=w_scales[m][:],
+                rhs=x_codes[v][:].bitcast(FP8X4),
+                rhs_scale=x_scales[v][:],
+                start=True,
+                stop=True,
             )
+            result = keep.tile([P, H], F32, name=f"result{m}{v}")
+            if on_scalar:
+                nc.scalar.activation(result[:], acc[m][v][:], IDENTITY, bias=bias[:, m : m + 1])
+            else:
+                nc.vector.tensor_scalar(result[:], acc[m][v][:], bias[:, m : m + 1], None, ADD)
+            nc.sync.dma_start(out[M * m : M * (m + 1), H * v : H * (v + 1)], result[:])
 
-        def w_slice(m):
-            return w_raw[m // 2][:, :, M * (m % 2) : M * (m % 2 + 1)]
-
-        interleave(nc.scalar.copy, x_grouped[0], looked[0][:])
-        interleave(nc.vector.tensor_copy, x_grouped[1], looked[1][:])
-        interleave(nc.scalar.copy, w_grouped[0], w_slice(0))
-        interleave(nc.scalar.copy, w_grouped[1], w_slice(1))
-        quantize(x_codes[0], x_scales[0], x_grouped[0])
-        quantize(x_codes[1], x_scales[1], x_grouped[1])
-        quantize(w_codes[0], w_scales[0], w_grouped[0])
-        interleave(nc.vector.tensor_copy, w_grouped[2], w_slice(2))
-        quantize(w_codes[1], w_scales[1], w_grouped[1])
-        interleave(nc.vector.tensor_copy, w_grouped[3], w_slice(3))
-        quantize(w_codes[2], w_scales[2], w_grouped[2])
-        quantize(w_codes[3], w_scales[3], w_grouped[3])
-
-        for m in range(4):
-            result = keep.tile([P, V], F32, name=f"result{m}")
-            for v in range(2):
-                acc = psum.tile([P, H], F32, name=f"acc{m}{v}")
-                nc.tensor.matmul_mx(
-                    out=acc[:],
-                    lhsT=w_codes[m][:].bitcast(FP8X4),
-                    lhsT_scale=w_scales[m][:],
-                    rhs=x_codes[v][:].bitcast(FP8X4),
-                    rhs_scale=x_scales[v][:],
-                    start=True,
-                    stop=True,
-                )
-                part = result[:, H * v : H * (v + 1)]
-                if v == 0:
-                    nc.scalar.activation(part, acc[:], IDENTITY, bias=bias[:, m : m + 1])
-                else:
-                    nc.vector.tensor_scalar(part, acc[:], bias[:, m : m + 1], None, ADD)
-            nc.sync.dma_start(out[M * m : M * (m + 1), :], result[:])
+        look_up(0, 0, H)
+        look_up(0, H, V)
+        look_up(1, 0, H)
+        group_x(nc.scalar.copy, 0, 0, H)
+        look_up(1, H, V)
+        group_x(nc.scalar.copy, 0, H, V)
+        look_up(2, 0, H)
+        look_up(3, 0, H)
+        group_x(nc.scalar.copy, 1, 0, H)
+        group_w(on_gpsimd, 0)
+        look_up(2, H, V)
+        look_up(3, H, V)
+        quantize_x(0)
+        quantize_w(0)
+        multiply(0, 0, True)
+        group_x(nc.scalar.copy, 1, H, V)
+        group_w(nc.vector.tensor_copy, 1)
+        group_w(nc.vector.tensor_copy, 2)
+        quantize_w(1)
+        multiply(1, 0, True)
+        quantize_x(1)
+        multiply(0, 1, True)
+        multiply(1, 1, True)
+        quantize_w(2)
+        group_w(nc.vector.tensor_copy, 3)
+        multiply(2, 0, True)
+        multiply(2, 1, True)
+        quantize_w(3)
+        multiply(3, 0, False)
+        multiply(3, 1, True)

from contextlib import ExitStack

import concourse.mybir as mybir
from concourse.masks import make_identity

K, T, LEVELS, V, N = 512, 1024, 4, 512, 512
FLOPS = 2 * K * N * V

F32 = mybir.dt.float32
BF16 = mybir.dt.bfloat16
U32 = mybir.dt.uint32
U16 = mybir.dt.uint16
U8 = mybir.dt.uint8
FP8X4 = mybir.dt.float8_e4m3fn_x4
ADD = mybir.AluOpType.add
MULT = mybir.AluOpType.mult
IDENTITY = mybir.ActivationFunctionType.Identity

P = 128
H = 256
M = 128


def tile_picked_grid_lin_bias_sub_l_kernel(tc, xT, w, b, offs, out):
    nc = tc.nc
    with ExitStack() as ctx:
        lists = ctx.enter_context(tc.tile_pool(name="lists", bufs=1))
        keep = ctx.enter_context(tc.tile_pool(name="keep", bufs=1))
        psum = ctx.enter_context(tc.psum_pool(name="psum", bufs=1))

        offsets = lists.tile([P, LEVELS * V // 16], U16, name="offsets")
        nc.sync.dma_start(offsets[:], offs)
        x_levels = xT.rearrange("(f l) t -> l f t", l=LEVELS)
        tables = []
        for l in range(LEVELS):
            table = keep.tile([P, T], F32, name=f"table{l}")
            nc.sync.dma_start(table[:], x_levels[l])
            tables.append(table)
        w_raw = []
        for h in range(2):
            raw = keep.tile([P, 4, 2 * M], F32, name=f"w_raw{h}")
            nc.sync.dma_start(raw[:], w[:, 2 * M * h : 2 * M * (h + 1)].rearrange("(p j) c -> p j c", j=4))
            w_raw.append(raw)

        acc = [[psum.tile([P, H], F32, name=f"acc{m}{v}") for v in range(2)] for m in range(4)]

        bias_rows = keep.tile([P, P], F32, name="bias_rows")
        nc.gpsimd.memset(bias_rows[:], 0.0)
        nc.scalar.dma_start(bias_rows[0:4, :], b.rearrange("(c m) o -> c (m o)", c=4))
        identity = keep.tile([P, P], F32, name="identity")
        make_identity(nc, identity[:])
        nc.tensor.transpose(acc[3][1][:, 0:P], bias_rows[:], identity[:])
        bias = keep.tile([P, 4], F32, name="bias")
        nc.scalar.activation(bias[:], acc[3][1][:, 0:4], IDENTITY)

        looked = [keep.tile([P, 2, V], F32, name=f"looked{i}") for i in range(2)]

        def look_up(l, v0, v1):
            first = (V * l + v0) // 16
            last = (V * l + v1) // 16
            nc.vector.tensor_copy(looked[l // 2][:, l % 2, v0:v1], tables[l][:].indirect(offsets[:, first:last]))

        x_grouped = keep.tile([P, V, 4], BF16, name="x_grouped", align_bytes=64)
        x_codes = [keep.tile([P, H], U32, name=f"x_codes{v}", align_bytes=64) for v in range(2)]
        x_scales = [keep.tile([P, H], U8, name=f"x_scales{v}", align_bytes=64) for v in range(2)]
        w_grouped = [keep.tile([P, M, 4], BF16, name=f"w_grouped{m}", align_bytes=64) for m in range(4)]
        w_codes = [keep.tile([P, M], U32, name=f"w_codes{m}", align_bytes=64) for m in range(4)]
        w_scales = [keep.tile([P, M], U8, name=f"w_scales{m}", align_bytes=64) for m in range(4)]

        def group_x(copy, i, v0, v1):
            copy(x_grouped[:, v0:v1, 2 * i : 2 * i + 2], looked[i][:, :, v0:v1].rearrange("p j n -> p n j"))

        def on_gpsimd(dst, src):
            nc.gpsimd.tensor_scalar(dst, src, 1.0, 0.0, MULT, ADD)

        def group_w(copy, m):
            raw = w_raw[m // 2][:, :, M * (m % 2) : M * (m % 2 + 1)]
            copy(w_grouped[m][:], raw.rearrange("p j n -> p n j"))

        def quantize(codes, scales, grouped):
            nc.vector.quantize_mx(out=codes[:].bitcast(FP8X4), scales=scales[:], in_=grouped.rearrange("p n j -> p (n j)"))

        def quantize_x(v):
            quantize(x_codes[v], x_scales[v], x_grouped[:, H * v : H * (v + 1), :])

        def quantize_w(m):
            quantize(w_codes[m], w_scales[m], w_grouped[m][:])

        def multiply(m, v, on_scalar):
            nc.tensor.matmul_mx(
                out=acc[m][v][:],
                lhsT=w_codes[m][:].bitcast(FP8X4),
                lhsT_scale=w_scales[m][:],
                rhs=x_codes[v][:].bitcast(FP8X4),
                rhs_scale=x_scales[v][:],
                start=True,
                stop=True,
            )
            result = keep.tile([P, H], F32, name=f"result{m}{v}")
            if on_scalar:
                nc.scalar.activation(result[:], acc[m][v][:], IDENTITY, bias=bias[:, m : m + 1])
            else:
                nc.vector.tensor_scalar(result[:], acc[m][v][:], bias[:, m : m + 1], None, ADD)
            nc.sync.dma_start(out[M * m : M * (m + 1), H * v : H * (v + 1)], result[:])

        look_up(0, 0, H)
        look_up(0, H, V)
        look_up(1, 0, H)
        group_x(nc.scalar.copy, 0, 0, H)
        look_up(1, H, V)
        group_x(nc.scalar.copy, 0, H, V)
        look_up(2, 0, H)
        look_up(3, 0, H)
        group_x(nc.scalar.copy, 1, 0, H)
        group_w(on_gpsimd, 0)
        look_up(2, H, V)
        look_up(3, H, V)
        quantize_x(0)
        quantize_w(0)
        multiply(0, 0, True)
        group_x(nc.scalar.copy, 1, H, V)
        group_w(nc.vector.tensor_copy, 1)
        group_w(nc.vector.tensor_copy, 2)
        quantize_w(1)
        multiply(1, 0, True)
        quantize_x(1)
        multiply(0, 1, True)
        multiply(1, 1, True)
        quantize_w(2)
        group_w(nc.vector.tensor_copy, 3)
        multiply(2, 0, True)
        multiply(2, 1, True)
        quantize_w(3)
        multiply(3, 0, False)
        multiply(3, 1, True)
